import numpy as np
CORES = [67,68,75,76,83,84,91,92,99,100,107,108,115,116,123,124]
N = 16
T = 256
ROUTE = [[[13,9,5],[6,8,9],[13,9,10],[3,1,5],[10,6,4],[4,7,2],[10,8,11],[6,13,10],[8,3,15],[6,10,15],[0,5,10],[7,15,9],[0,10,4],[14,0,12],[10,0,12],[12,8,7],[10,2,4],[11,9,0],[10,4,8],[10,3,13],[12,8,11],[7,15,13],[12,8,6],[3,12,9],[13,5,3],[11,5,0],[4,3,8],[10,13,0],[9,2,7],[12,2,3],[6,0,9],[13,11,4],[4,9,11],[9,7,10],[10,3,1],[2,14,4],[7,1,3],[9,13,3],[7,8,14],[0,11,10],[13,8,12],[15,3,7],[15,10,0],[10,14,5],[8,14,9],[12,14,9],[4,13,6],[6,3,15],[2,4,11],[15,10,0],[0,8,3],[0,15,10],[13,8,14],[15,4,1],[9,1,8],[15,3,7],[0,3,8],[10,12,8],[3,0,12],[15,3,0],[11,1,15],[4,7,8],[3,14,7],[15,7,5],[5,13,1],[2,3,12],[11,8,0],[10,0,7],[5,13,3],[12,4,8],[13,1,6],[2,15,8],[8,2,7],[15,9,12],[10,13,7],[10,7,3],[11,4,12],[15,4,12],[4,5,11],[11,2,0],[14,9,5],[0,3,8],[9,12,10],[9,15,10],[2,0,6],[13,10,3],[1,5,11],[11,12,10],[2,3,6],[13,8,12],[4,5,9],[1,13,2],[2,10,0],[10,2,0],[12,9,14],[0,1,12],[3,14,12],[6,12,3],[14,9,12],[9,13,6],[13,2,5],[6,3,8],[11,4,5],[13,14,11],[4,8,1],[7,10,1],[14,10,3],[13,8,2],[14,4,9],[14,7,8],[4,8,2],[3,0,13],[9,8,0],[1,14,11],[10,8,13],[2,15,13],[0,10,15],[15,0,8],[0,8,15],[8,15,0],[8,2,6],[15,11,13],[1,6,0],[6,14,7],[6,9,8],[12,1,13],[13,2,4],[8,2,9],[5,1,2],[4,11,5],[12,13,10],[3,5,12],[6,11,7],[3,4,15],[9,8,7],[11,2,0],[4,5,12],[11,2,9],[3,8,4],[13,5,12],[14,5,10],[15,9,4],[0,2,4],[9,0,2],[2,1,10],[9,4,11],[15,13,3],[1,5,9],[1,6,9],[12,3,2],[9,11,8],[6,12,8],[7,14,6],[8,3,14],[15,14,10],[1,2,0],[12,14,9],[10,8,4],[6,3,9],[4,3,7],[14,9,0],[9,8,4],[4,8,1],[12,2,13],[4,13,6],[4,2,8],[14,13,8],[3,1,11],[11,5,8],[6,11,8],[11,9,0],[10,3,14],[7,13,14],[15,6,4],[5,12,0],[1,6,10],[13,14,11],[9,11,4],[4,14,5],[14,8,1],[0,6,10],[15,12,1],[10,15,5],[6,13,10],[4,8,12],[14,9,5],[15,0,10],[12,0,7],[15,7,8],[5,1,14],[2,4,6],[12,9,15],[0,5,13],[8,1,14],[10,15,1],[7,14,1],[4,13,8],[3,13,9],[9,11,1],[13,15,7],[6,3,0],[5,7,10],[3,2,14],[5,10,9],[3,1,7],[2,4,7],[9,5,6],[0,6,2],[10,11,3],[8,11,5],[3,0,2],[0,9,8],[1,12,14],[4,9,5],[6,9,1],[11,14,6],[11,8,1],[3,0,12],[14,3,8],[7,4,14],[9,1,8],[2,1,9],[9,15,7],[2,11,3],[12,4,2],[7,10,9],[14,8,12],[8,6,15],[10,14,11],[4,8,9],[10,7,13],[6,2,12],[2,7,15],[7,6,12],[3,4,5],[1,7,3],[15,2,7],[1,5,9],[4,11,9],[2,0,12],[0,8,11],[10,0,14],[9,11,4],[13,14,2],[0,5,1],[3,1,2],[10,7,11],[11,6,1],[4,14,15],[15,2,5],[3,0,15],[15,1,9],[15,4,5],[2,3,9],[15,2,0],[6,15,7]],[[4,5,9],[14,7,3],[2,14,0],[10,9,13],[12,7,4],[10,6,7],[0,11,7],[10,3,7],[8,2,1],[5,1,4],[13,11,5],[4,8,11],[4,0,14],[1,3,15],[0,1,7],[4,3,8],[13,3,15],[1,15,7],[10,12,8],[7,2,13],[4,8,2],[12,0,3],[5,9,11],[2,9,0],[13,4,1],[9,11,12],[11,5,9],[15,10,12],[7,14,11],[12,2,6],[12,0,8],[2,9,8],[5,6,11],[3,8,11],[11,7,8],[9,10,5],[11,0,10],[9,15,7],[12,9,8],[5,9,15],[10,13,8],[9,6,1],[12,6,2],[10,9,5],[9,2,0],[2,0,14],[9,5,0],[14,0,1],[11,1,7],[11,7,4],[13,6,14],[6,14,5],[12,9,4],[6,7,8],[3,14,8],[14,10,12],[2,1,8],[11,7,8],[9,12,7],[2,11,13],[3,9,14],[12,14,9],[12,6,9],[10,9,8],[13,8,10],[0,11,12],[5,4,11],[13,9,14],[5,12,6],[7,3,1],[13,12,10],[7,14,6],[1,6,10],[0,6,7],[0,2,1],[13,4,1],[2,10,14],[2,8,11],[0,13,12],[3,13,5],[10,1,3],[9,11,13],[6,14,13],[7,13,1],[7,5,15],[15,4,13],[6,12,7],[14,8,12],[2,13,1],[14,0,13],[9,7,3],[11,15,2],[0,15,9],[0,9,6],[10,14,9],[12,11,2],[4,11,12],[15,12,13],[10,13,6],[2,3,4],[2,6,11],[7,4,2],[5,6,9],[8,1,3],[13,2,10],[15,4,10],[9,3,1],[0,1,9],[6,0,14],[5,14,9],[12,5,7],[6,1,0],[1,9,2],[2,12,1],[15,11,12],[9,11,3],[0,9,5],[11,10,13],[1,7,8],[2,10,5],[2,7,1],[11,8,9],[2,12,0],[15,4,0],[5,15,2],[3,0,10],[5,9,11],[14,5,3],[6,7,1],[3,1,13],[10,14,11],[11,10,1],[5,15,2],[10,2,1],[11,5,1],[9,5,14],[7,4,9],[12,8,1],[0,15,7],[9,13,1],[4,11,2],[12,10,6],[15,14,1],[12,0,4],[2,11,13],[1,2,6],[6,1,2],[8,5,4],[2,1,7],[11,6,13],[11,2,8],[2,8,15],[2,9,13],[10,14,0],[9,4,8],[5,12,1],[14,2,11],[12,9,14],[1,7,11],[5,11,15],[7,10,9],[4,15,11],[1,4,12],[3,2,8],[3,10,14],[0,12,6],[7,2,6],[12,5,1],[4,13,5],[8,4,1],[0,7,12],[2,8,15],[3,13,8],[5,9,1],[15,9,2],[7,2,13],[9,2,1],[3,1,5],[13,9,10],[12,8,3],[8,0,6],[15,12,1],[3,5,15],[2,8,13],[5,11,15],[2,4,13],[12,9,14],[3,9,15],[6,4,1],[13,5,4],[14,10,9],[3,12,7],[11,15,2],[10,15,4],[15,7,14],[2,4,10],[7,1,2],[7,11,9],[0,2,12],[9,8,14],[13,5,2],[14,11,0],[14,11,15],[7,2,6],[11,1,13],[6,13,8],[2,14,13],[12,3,8],[14,3,5],[2,9,3],[14,4,10],[14,15,6],[7,14,0],[2,10,12],[3,8,9],[15,8,2],[7,6,5],[2,13,8],[12,6,11],[7,9,8],[13,4,9],[10,2,6],[2,8,12],[12,9,13],[9,7,13],[5,13,14],[8,1,6],[15,13,2],[4,7,9],[12,10,13],[6,12,13],[4,1,10],[6,1,15],[15,3,6],[3,6,4],[14,15,7],[0,14,10],[3,13,11],[3,15,6],[14,10,8],[11,4,1],[5,4,10],[10,14,1],[8,1,15],[3,6,5],[4,15,10],[1,4,2],[7,5,14],[2,9,6],[10,14,6],[4,12,5],[3,5,15],[2,15,3],[11,8,13],[3,1,13],[11,4,15]],[[10,9,4],[13,3,2],[13,0,7],[5,7,3],[10,4,7],[8,13,7],[12,15,6],[0,5,1],[6,14,10],[15,2,13],[13,8,5],[4,7,10],[5,2,1],[0,10,14],[12,7,13],[1,0,15],[3,11,2],[7,6,8],[2,7,12],[0,15,9],[13,7,9],[11,14,4],[2,9,14],[14,1,10],[5,1,15],[7,8,2],[14,7,0],[12,13,5],[15,5,11],[13,12,0],[5,9,10],[9,15,5],[1,7,9],[8,6,12],[13,7,1],[4,6,0],[6,4,10],[2,4,13],[8,11,13],[11,15,0],[8,13,12],[14,3,12],[5,15,9],[15,14,5],[9,4,5],[7,2,6],[10,2,12],[6,1,13],[14,12,5],[14,6,5],[3,0,13],[13,11,2],[3,8,14],[3,1,0],[11,2,6],[1,6,3],[5,7,12],[9,13,3],[2,11,10],[12,0,15],[15,3,8],[14,8,15],[10,14,3],[12,0,3],[3,1,14],[9,15,13],[11,9,2],[13,11,3],[3,8,10],[13,9,4],[0,4,1],[4,14,10],[13,15,1],[7,6,3],[3,13,2],[14,15,13],[5,9,8],[14,0,2],[2,8,13],[14,7,10],[8,14,5],[12,14,13],[11,10,14],[14,2,1],[7,14,11],[3,7,13],[3,14,12],[1,10,7],[4,13,15],[2,6,3],[1,14,5],[6,13,7],[0,11,15],[4,0,10],[14,13,8],[0,13,14],[0,2,1],[4,7,5],[14,6,5],[9,10,0],[9,2,14],[0,7,10],[2,12,6],[4,10,12],[0,9,5],[2,4,5],[9,10,13],[11,9,0],[14,11,0],[11,7,8],[9,8,1],[7,11,3],[13,11,12],[5,0,7],[14,12,11],[15,1,11],[11,7,14],[6,14,13],[0,1,4],[3,5,2],[9,0,5],[3,2,4],[9,6,14],[8,13,9],[13,1,12],[14,11,4],[11,9,1],[6,13,15],[1,10,15],[7,4,15],[7,10,14],[6,7,5],[1,11,2],[15,4,12],[2,1,15],[9,13,2],[7,8,10],[4,6,0],[4,0,7],[1,3,12],[9,2,8],[10,14,3],[8,4,2],[3,9,8],[9,15,0],[9,0,3],[5,8,1],[2,15,11],[6,13,1],[4,10,5],[9,11,8],[15,2,11],[15,12,10],[14,2,9],[14,10,5],[11,3,4],[5,1,12],[0,3,12],[15,0,3],[8,10,7],[2,9,1],[1,4,9],[14,15,6],[15,8,13],[15,6,9],[6,13,10],[2,5,11],[10,15,14],[1,9,13],[15,14,7],[7,5,6],[8,1,4],[11,8,0],[1,4,9],[13,15,9],[11,12,1],[0,4,15],[8,12,3],[10,0,15],[10,1,15],[12,15,6],[12,15,14],[11,6,2],[5,8,9],[2,15,4],[8,3,9],[1,13,12],[9,13,7],[10,14,5],[3,12,2],[11,7,15],[5,2,11],[3,2,0],[6,14,1],[5,14,4],[6,3,1],[7,3,10],[12,9,13],[14,0,4],[1,7,10],[15,5,8],[13,4,11],[13,8,12],[15,0,6],[15,14,5],[2,7,11],[4,0,12],[0,6,9],[11,7,5],[9,14,15],[2,9,7],[8,3,12],[8,6,13],[15,14,13],[5,0,15],[3,13,15],[2,10,1],[1,7,0],[4,0,6],[3,7,10],[10,14,15],[8,9,6],[5,15,3],[11,12,6],[4,8,5],[3,12,7],[11,6,8],[6,8,11],[15,8,4],[11,8,10],[4,0,3],[13,7,15],[15,1,7],[1,14,11],[13,5,10],[4,14,9],[11,9,6],[7,0,2],[1,5,13],[4,11,0],[2,7,15],[2,15,1],[4,2,5],[9,8,1],[3,9,7],[4,9,14],[0,14,12],[5,4,10],[11,14,15],[8,5,6],[12,15,13],[5,6,4],[4,8,6],[6,9,14],[8,12,3],[15,2,6]],[[13,10,9],[8,3,1],[14,5,4],[7,13,1],[10,3,5],[2,1,3],[7,12,1],[8,7,13],[9,0,2],[6,14,13],[15,1,10],[8,13,0],[10,4,9],[7,2,12],[9,5,14],[14,15,13],[2,1,12],[1,0,6],[4,5,7],[10,3,13],[8,0,9],[0,1,5],[0,14,5],[11,7,0],[12,2,9],[5,1,13],[0,5,13],[2,7,5],[10,0,5],[1,11,4],[14,4,15],[9,4,7],[1,8,0],[3,13,0],[12,15,10],[14,8,2],[11,5,4],[7,14,15],[10,8,15],[13,9,4],[11,4,15],[3,12,0],[1,11,6],[3,4,11],[9,0,13],[11,13,10],[0,12,11],[6,10,13],[12,8,3],[12,15,6],[13,14,10],[8,5,15],[0,10,13],[15,9,14],[14,3,13],[3,4,11],[9,15,10],[6,13,11],[15,4,10],[2,4,0],[5,15,1],[5,15,14],[10,4,15],[4,1,7],[5,11,2],[5,6,11],[15,12,8],[9,11,3],[3,2,13],[4,0,6],[7,14,2],[7,15,11],[15,0,10],[3,15,12],[5,11,12],[4,7,11],[12,11,8],[15,14,3],[1,9,12],[2,15,11],[12,11,8],[6,9,1],[14,12,4],[4,11,13],[12,9,0],[13,3,9],[11,9,0],[2,8,4],[14,3,10],[13,2,1],[3,15,11],[9,14,15],[7,14,15],[6,10,0],[4,11,7],[14,12,2],[1,6,3],[3,7,5],[6,0,15],[11,14,12],[8,6,3],[6,14,13],[14,2,15],[8,10,11],[8,12,2],[10,13,11],[5,6,9],[7,10,6],[14,0,8],[6,8,15],[1,13,15],[12,0,9],[7,4,9],[13,4,5],[14,15,4],[13,11,12],[11,12,7],[8,15,1],[11,13,14],[14,11,2],[7,12,15],[6,1,2],[5,6,0],[3,2,5],[6,12,3],[6,12,8],[9,11,10],[11,12,2],[8,13,5],[9,3,5],[5,8,2],[10,8,4],[11,7,0],[1,0,4],[7,8,12],[15,1,2],[9,12,6],[4,8,2],[4,13,6],[8,14,3],[1,13,12],[6,2,7],[6,1,9],[4,13,5],[12,14,11],[1,8,11],[13,14,15],[6,13,1],[6,1,13],[11,8,9],[0,15,7],[1,8,4],[12,4,13],[13,12,2],[5,4,15],[14,15,8],[2,9,12],[15,9,7],[6,10,14],[4,14,2],[15,0,12],[7,6,0],[9,0,1],[8,9,3],[11,7,4],[3,2,4],[3,9,8],[10,9,7],[5,2,12],[12,0,5],[0,13,15],[13,11,2],[7,0,8],[4,2,15],[3,9,2],[7,11,6],[2,15,10],[12,5,1],[4,12,9],[4,12,6],[15,7,12],[11,2,5],[13,6,1],[2,9,12],[2,7,10],[12,3,6],[15,11,12],[13,11,14],[11,5,6],[7,5,2],[5,10,9],[7,1,3],[9,12,0],[4,0,12],[12,11,3],[5,11,1],[7,8,12],[11,1,5],[10,13,3],[10,4,13],[15,13,8],[12,4,14],[0,11,6],[5,11,12],[0,1,12],[3,5,4],[14,4,9],[11,14,4],[0,3,11],[6,11,15],[7,10,6],[9,7,4],[10,13,0],[9,2,0],[7,5,10],[10,0,9],[0,6,9],[11,13,7],[0,2,11],[1,14,2],[12,14,7],[9,3,14],[13,10,12],[11,5,2],[5,15,13],[10,11,14],[12,0,6],[8,7,0],[10,1,0],[15,5,0],[2,12,13],[15,4,0],[14,6,5],[1,7,3],[3,7,6],[6,10,14],[1,13,11],[7,4,6],[1,8,2],[7,14,2],[10,8,12],[13,10,3],[10,0,12],[5,4,1],[4,10,2],[12,7,3],[4,11,2],[6,13,5],[7,9,3],[9,13,1],[15,13,4],[1,14,7],[0,10,4],[1,0,8],[11,1,15],[3,1,7]],[[0,8,13],[2,5,14],[9,13,8],[10,4,11],[0,1,8],[13,5,7],[4,14,12],[2,11,15],[1,8,6],[7,12,14],[5,1,7],[5,13,0],[13,11,12],[14,10,11],[1,4,14],[8,4,2],[14,8,13],[4,12,13],[13,8,15],[14,8,5],[2,1,7],[15,13,4],[0,12,11],[6,7,11],[15,9,13],[13,6,11],[5,6,12],[14,15,0],[12,8,9],[0,2,3],[8,7,6],[9,14,3],[11,2,3],[5,4,12],[11,15,10],[12,14,3],[13,1,5],[12,15,6],[3,13,9],[0,5,1],[6,1,3],[10,7,3],[11,3,5],[5,1,7],[0,7,2],[13,10,3],[12,0,4],[0,7,8],[7,1,5],[8,11,2],[12,9,0],[2,11,13],[13,9,12],[12,7,4],[11,4,12],[6,0,2],[12,2,10],[3,5,7],[8,0,2],[14,5,8],[13,2,9],[5,13,14],[6,4,9],[7,10,9],[2,7,5],[12,9,4],[1,12,14],[3,15,1],[1,14,13],[9,8,7],[12,9,15],[7,3,10],[11,8,2],[5,0,13],[2,1,15],[0,3,10],[13,12,15],[13,12,8],[3,8,1],[3,7,10],[9,10,12],[5,15,3],[12,6,0],[5,11,4],[0,10,4],[13,1,0],[15,13,6],[15,6,12],[10,13,5],[5,1,12],[2,3,6],[8,3,1],[15,1,12],[7,2,15],[1,14,15],[10,5,13],[13,1,12],[6,15,4],[15,9,8],[9,7,4],[9,13,1],[5,13,11],[15,4,11],[11,6,14],[7,4,3],[11,7,13],[1,15,6],[7,10,2],[7,9,5],[7,4,5],[1,14,11],[5,4,1],[11,5,15],[12,11,14],[12,11,3],[12,15,0],[4,7,13],[3,14,6],[12,14,2],[14,9,8],[12,13,8],[7,9,3],[2,10,1],[6,3,4],[5,15,13],[6,7,11],[3,13,15],[0,5,6],[5,2,14],[12,7,3],[3,2,7],[4,9,15],[0,15,8],[0,3,6],[8,9,7],[8,11,13],[12,13,15],[0,2,13],[15,6,13],[12,3,8],[12,3,2],[15,6,10],[5,15,14],[14,10,7],[2,13,3],[7,9,10],[0,13,4],[5,4,2],[3,7,4],[10,7,5],[8,1,6],[8,9,7],[10,1,14],[3,5,7],[6,10,13],[8,5,7],[10,4,6],[1,13,10],[3,8,6],[12,11,15],[5,11,14],[15,14,0],[8,4,15],[7,9,1],[7,2,0],[3,9,5],[5,8,7],[1,14,15],[7,11,15],[8,0,2],[7,3,12],[8,12,0],[3,1,2],[9,7,13],[9,10,12],[0,3,10],[6,2,15],[9,7,3],[14,0,3],[8,7,3],[11,2,14],[4,12,11],[1,0,3],[15,6,10],[4,6,5],[4,11,2],[15,8,10],[9,13,10],[15,6,4],[9,14,6],[8,11,10],[12,7,0],[3,14,8],[10,5,8],[5,8,10],[10,3,12],[13,0,1],[8,13,14],[7,6,10],[4,5,11],[14,1,2],[12,8,15],[3,4,9],[1,2,8],[12,9,3],[10,6,0],[9,8,13],[9,14,1],[0,6,7],[15,8,13],[13,4,12],[1,4,8],[15,9,7],[12,4,3],[13,2,7],[3,1,9],[4,6,11],[13,1,2],[6,13,2],[0,2,4],[14,6,5],[10,9,2],[14,7,6],[15,13,1],[3,12,0],[8,14,3],[0,6,7],[5,8,9],[5,4,7],[4,15,5],[12,6,10],[4,7,12],[12,0,5],[13,3,6],[5,0,10],[2,3,6],[10,3,2],[3,7,12],[15,3,6],[5,0,2],[13,1,5],[12,9,5],[3,1,8],[11,0,5],[8,3,13],[6,15,11],[14,4,0],[15,14,6],[11,9,5],[3,7,12],[13,3,8],[2,8,1],[5,12,2],[13,4,8],[14,4,11],[3,12,13]],[[13,7,11],[10,12,13],[6,10,9],[15,0,6],[7,4,14],[4,5,6],[0,6,4],[5,11,9],[12,5,2],[15,14,10],[9,8,11],[4,13,2],[1,7,13],[8,5,1],[5,1,0],[5,0,11],[3,15,5],[8,0,12],[6,5,4],[6,13,0],[8,11,6],[13,14,5],[2,3,4],[6,12,14],[14,3,6],[13,7,12],[6,12,8],[12,0,8],[12,13,9],[6,0,13],[3,15,7],[12,3,14],[5,2,13],[10,0,2],[11,14,6],[14,10,11],[3,11,0],[5,4,2],[12,13,2],[0,8,13],[14,5,2],[10,2,0],[12,11,8],[11,7,10],[10,5,9],[1,10,6],[7,0,11],[1,8,15],[4,6,2],[3,5,15],[11,12,9],[9,3,12],[4,9,1],[14,3,0],[1,8,10],[10,12,0],[3,7,15],[0,10,8],[9,2,13],[15,2,8],[5,3,7],[1,0,2],[12,4,5],[6,8,15],[12,5,10],[7,1,15],[10,7,0],[13,12,7],[6,11,15],[11,8,0],[14,13,0],[5,12,0],[14,1,11],[10,8,2],[5,15,11],[14,1,3],[3,2,1],[14,1,9],[8,11,3],[11,13,2],[3,14,9],[3,7,13],[15,11,3],[14,2,11],[0,5,9],[10,3,2],[0,1,10],[11,13,4],[11,4,7],[7,10,13],[15,10,11],[1,4,15],[10,5,14],[4,0,14],[9,11,2],[9,14,15],[14,8,6],[8,11,12],[9,13,4],[4,11,7],[8,3,10],[8,11,3],[15,8,10],[8,11,10],[13,4,14],[1,11,14],[0,8,13],[9,4,14],[7,12,6],[1,0,14],[10,4,6],[9,8,11],[14,5,3],[2,12,13],[2,8,5],[8,4,5],[10,14,13],[1,14,13],[7,10,13],[7,0,13],[13,11,7],[9,7,1],[14,4,13],[5,11,6],[8,0,5],[13,9,15],[1,15,10],[14,1,11],[0,3,12],[0,7,3],[4,5,8],[15,11,7],[8,15,14],[7,15,0],[2,0,6],[15,12,4],[2,15,9],[4,15,5],[11,10,6],[0,4,9],[14,2,6],[13,3,6],[13,6,9],[1,11,3],[7,10,8],[3,1,4],[0,4,12],[1,0,4],[0,8,2],[10,11,0],[15,10,12],[5,6,7],[15,11,5],[6,0,4],[1,0,9],[3,14,8],[9,10,8],[2,0,5],[15,8,10],[7,11,14],[0,1,3],[6,4,9],[9,2,12],[3,13,14],[1,8,7],[1,6,9],[10,15,14],[7,11,15],[1,6,9],[7,5,15],[14,12,6],[5,10,12],[5,10,13],[13,7,14],[15,8,3],[12,10,4],[11,0,13],[11,8,14],[0,5,14],[8,3,10],[9,0,15],[4,5,14],[3,1,8],[14,10,5],[5,8,9],[12,8,10],[1,0,7],[13,0,10],[12,7,8],[5,10,9],[0,13,5],[11,7,13],[4,5,12],[11,7,4],[4,1,8],[6,8,2],[12,11,9],[7,8,15],[1,13,14],[9,1,6],[3,15,14],[15,10,5],[6,13,9],[8,9,3],[0,14,5],[2,15,10],[0,1,8],[2,5,8],[12,14,2],[9,2,3],[11,8,9],[9,8,3],[6,2,14],[12,3,8],[1,0,9],[2,4,13],[14,8,12],[10,6,5],[14,9,7],[7,10,9],[0,12,2],[14,5,9],[3,7,12],[15,3,11],[7,8,6],[5,12,10],[14,9,6],[13,14,9],[4,7,11],[15,4,9],[4,13,12],[8,7,6],[2,9,1],[0,3,12],[11,5,2],[8,5,3],[10,5,7],[3,2,6],[14,2,0],[4,14,9],[10,2,6],[1,14,6],[5,4,3],[1,7,12],[14,11,15],[15,0,8],[15,3,14],[2,5,8],[10,14,12],[4,9,7],[3,14,15],[0,6,1],[4,7,1],[3,11,13],[7,12,5],[7,3,9]],[[12,6,11],[12,13,4],[2,3,14],[8,2,1],[12,15,6],[6,1,8],[14,12,7],[3,14,13],[7,9,1],[13,14,7],[15,7,6],[5,1,4],[11,10,15],[4,6,3],[2,13,1],[0,3,7],[10,15,0],[3,7,6],[1,15,14],[7,13,2],[12,13,0],[4,2,13],[3,4,8],[11,7,13],[15,6,8],[7,4,10],[8,9,4],[9,0,1],[2,14,15],[7,14,15],[1,10,13],[15,4,3],[0,7,1],[0,10,14],[2,11,0],[1,6,5],[2,1,13],[6,12,7],[1,14,10],[7,9,8],[6,0,8],[12,7,11],[7,5,8],[9,3,13],[14,8,11],[2,14,13],[0,13,12],[0,14,4],[1,12,11],[7,5,14],[13,0,14],[15,5,2],[0,12,7],[0,1,8],[11,3,10],[10,9,2],[1,2,5],[7,14,15],[2,7,4],[6,11,5],[1,3,0],[8,12,1],[7,5,4],[2,12,5],[12,14,3],[2,14,13],[8,3,11],[8,9,14],[8,6,7],[15,14,13],[14,8,5],[9,8,3],[2,1,15],[6,9,5],[7,5,10],[4,8,5],[3,0,14],[10,12,8],[11,2,4],[13,3,4],[7,14,15],[5,3,14],[1,11,0],[14,6,3],[8,11,7],[1,15,8],[12,8,0],[1,2,3],[7,5,10],[6,13,11],[7,10,2],[10,14,0],[6,5,3],[11,15,6],[4,7,5],[9,12,15],[8,12,2],[12,9,4],[10,8,7],[1,15,10],[11,15,12],[10,3,2],[13,12,4],[1,7,0],[14,15,9],[15,2,11],[13,12,15],[10,7,4],[4,2,8],[2,1,15],[6,15,1],[2,10,15],[2,11,7],[13,12,1],[7,2,9],[15,4,8],[1,9,13],[6,8,4],[6,13,5],[0,14,10],[0,11,15],[4,11,14],[6,14,9],[3,5,8],[15,5,2],[5,14,10],[10,15,9],[2,3,7],[12,7,8],[4,11,6],[6,2,9],[14,9,6],[8,4,14],[13,0,1],[1,9,0],[9,5,3],[9,1,8],[7,13,14],[7,11,9],[1,3,0],[3,4,15],[8,4,11],[12,15,13],[8,5,13],[6,8,0],[8,13,12],[3,5,7],[13,0,10],[9,3,14],[6,7,15],[9,10,8],[15,4,13],[0,12,14],[11,1,4],[12,4,15],[10,12,8],[8,13,2],[13,6,4],[11,2,15],[0,2,13],[5,10,8],[4,1,9],[11,10,0],[4,9,13],[0,14,8],[9,5,2],[13,14,12],[0,3,8],[5,11,6],[4,2,8],[6,8,2],[6,5,12],[13,9,2],[1,15,2],[2,13,5],[2,6,13],[3,13,5],[4,0,8],[2,1,13],[9,7,5],[3,13,4],[7,15,8],[3,13,12],[5,2,0],[7,15,6],[5,4,9],[8,7,15],[12,6,7],[7,4,8],[6,10,5],[5,0,4],[3,10,2],[12,10,5],[7,2,13],[0,8,13],[2,5,6],[14,4,9],[6,7,10],[9,5,2],[9,3,4],[14,7,15],[9,2,10],[9,7,14],[4,15,7],[1,6,13],[11,1,6],[0,7,11],[14,1,0],[6,4,5],[12,13,6],[14,12,1],[15,6,8],[13,8,0],[6,5,1],[11,4,8],[13,9,11],[12,3,15],[2,4,11],[11,5,12],[5,2,1],[15,0,13],[2,13,15],[3,0,2],[11,1,15],[10,4,15],[13,10,6],[12,2,4],[5,10,6],[12,5,4],[9,13,8],[11,14,8],[4,3,2],[12,10,0],[11,14,10],[9,2,13],[1,9,10],[2,5,11],[4,10,5],[4,1,6],[9,6,11],[8,3,7],[0,6,14],[8,12,3],[8,9,1],[4,13,5],[11,1,4],[7,6,2],[15,2,7],[1,5,10],[1,5,11],[1,13,8],[3,10,14],[4,9,13],[1,11,4],[2,15,1],[8,3,7]],[[3,8,5],[11,4,13],[13,5,8],[0,15,13],[14,11,13],[15,5,0],[10,14,6],[2,1,9],[11,14,15],[4,6,14],[15,11,4],[6,0,10],[13,10,14],[9,3,10],[2,1,9],[4,10,12],[13,12,1],[9,10,3],[6,9,10],[9,5,13],[7,9,11],[14,5,15],[0,11,8],[12,6,11],[13,15,11],[13,15,14],[0,4,6],[2,6,11],[12,2,13],[13,4,7],[1,13,4],[7,9,10],[4,1,9],[11,1,4],[3,11,7],[6,12,1],[5,4,14],[7,12,10],[6,5,11],[2,10,11],[6,2,5],[7,11,8],[1,4,15],[6,12,14],[5,11,6],[12,5,8],[0,7,6],[12,1,7],[11,13,0],[3,4,0],[1,5,7],[3,11,10],[0,10,11],[4,10,6],[2,13,11],[15,6,5],[13,7,8],[6,12,0],[5,0,1],[12,2,7],[1,7,14],[1,4,14],[4,2,10],[8,11,0],[8,14,7],[1,8,13],[2,4,1],[2,14,11],[6,12,10],[12,15,6],[13,8,15],[3,13,8],[1,3,14],[6,12,3],[11,4,13],[6,9,5],[0,12,6],[0,1,5],[0,13,2],[1,4,14],[15,13,9],[10,12,0],[1,12,10],[12,9,11],[7,10,11],[7,5,15],[3,8,7],[7,12,9],[2,7,4],[2,14,7],[7,5,14],[0,11,9],[4,11,6],[7,13,12],[2,10,13],[9,15,14],[5,15,4],[12,1,10],[13,1,8],[8,0,15],[11,10,13],[11,7,12],[9,6,8],[5,15,9],[9,4,11],[7,6,2],[6,11,8],[11,12,5],[3,10,11],[6,0,14],[7,15,12],[3,15,11],[14,12,3],[6,15,2],[11,2,6],[4,12,1],[2,1,11],[12,5,10],[2,4,6],[9,7,11],[2,1,15],[1,3,0],[8,15,4],[12,13,3],[14,12,9],[9,3,8],[8,14,5],[12,3,0],[15,12,0],[5,14,1],[4,13,14],[10,0,6],[15,7,3],[9,8,10],[2,13,0],[5,8,0],[9,5,8],[10,2,12],[0,9,15],[5,12,6],[13,3,14],[1,9,11],[8,11,4],[9,8,14],[4,8,11],[8,0,14],[7,11,4],[5,7,15],[8,13,2],[11,10,0],[11,10,6],[8,4,3],[14,15,13],[7,12,4],[5,12,10],[7,14,9],[14,13,3],[8,2,13],[12,14,1],[3,5,11],[13,11,10],[9,7,13],[13,15,11],[2,8,1],[12,4,14],[5,6,3],[15,2,0],[10,4,14],[11,7,1],[3,0,9],[8,9,7],[10,8,12],[14,2,15],[13,8,2],[6,7,4],[13,14,10],[10,4,9],[6,0,11],[8,6,1],[14,9,2],[8,12,9],[8,3,5],[13,14,4],[0,4,3],[14,1,11],[6,14,9],[11,6,1],[14,1,9],[15,11,1],[14,13,15],[9,6,0],[13,3,2],[4,8,9],[13,0,9],[7,1,3],[14,8,15],[2,4,9],[3,5,7],[11,3,12],[2,12,7],[6,3,11],[1,7,8],[5,6,12],[6,13,8],[4,1,7],[9,15,13],[11,0,14],[1,0,6],[15,5,12],[14,1,6],[5,9,11],[12,0,3],[1,13,2],[13,15,1],[6,0,15],[4,13,8],[6,14,5],[12,0,4],[11,6,9],[7,3,10],[4,14,15],[9,11,7],[13,4,5],[15,7,10],[4,14,7],[1,15,3],[7,10,6],[5,2,13],[10,2,0],[11,3,0],[3,11,14],[11,4,2],[9,10,2],[9,5,0],[9,2,10],[6,11,14],[5,2,6],[11,13,10],[0,6,12],[2,7,10],[7,3,14],[2,4,14],[5,12,9],[2,4,0],[2,9,12],[15,3,7],[9,11,6],[13,2,3],[2,7,3],[14,12,9],[3,15,6],[2,5,9],[6,3,11],[14,10,8],[15,11,12],[10,9,13]],[[5,10,8],[13,3,8],[8,9,1],[10,13,6],[14,15,3],[7,9,0],[1,12,2],[8,10,7],[0,15,7],[12,1,0],[7,8,1],[5,1,10],[15,7,13],[11,10,12],[1,3,8],[1,9,6],[0,11,13],[3,12,6],[3,13,6],[15,7,11],[4,14,3],[8,1,12],[3,13,10],[6,7,13],[9,7,5],[13,1,4],[5,0,1],[1,6,4],[4,6,8],[15,4,13],[0,15,2],[11,8,2],[4,8,14],[7,13,6],[3,1,2],[1,0,2],[14,2,9],[4,7,11],[11,9,0],[2,14,15],[8,2,0],[6,9,2],[15,3,7],[4,14,2],[10,13,5],[15,13,4],[6,10,3],[14,13,10],[11,12,10],[13,12,10],[3,5,10],[0,6,11],[6,15,5],[7,5,2],[3,12,9],[5,13,1],[1,8,5],[4,1,14],[4,11,2],[2,4,15],[7,11,9],[8,13,5],[5,9,14],[14,12,5],[4,12,10],[3,2,15],[8,6,14],[2,10,8],[8,3,14],[6,9,14],[4,11,6],[4,14,3],[12,3,14],[2,7,5],[0,15,1],[6,15,2],[12,6,7],[7,1,13],[2,13,1],[10,1,15],[12,7,8],[8,7,0],[7,12,0],[2,12,10],[5,10,12],[10,8,13],[8,13,14],[1,0,10],[3,9,5],[5,6,10],[9,13,5],[15,3,13],[1,9,3],[5,0,12],[9,14,12],[13,4,15],[8,7,2],[3,2,10],[8,14,3],[6,14,12],[2,3,10],[8,11,13],[7,4,13],[8,14,15],[15,6,2],[3,14,10],[15,13,5],[7,2,15],[6,7,8],[12,13,8],[15,1,9],[8,15,1],[5,15,8],[5,8,11],[12,4,3],[1,12,8],[10,4,11],[9,0,1],[4,15,10],[4,14,9],[0,14,8],[0,9,3],[3,0,14],[1,8,3],[12,14,5],[13,12,4],[5,2,14],[5,7,14],[4,8,9],[14,2,7],[1,2,14],[8,15,12],[6,11,13],[9,8,12],[1,14,15],[10,4,5],[14,2,15],[1,0,5],[9,4,3],[14,7,2],[12,3,0],[14,13,4],[12,1,2],[14,5,9],[12,11,1],[11,13,12],[15,13,1],[14,4,0],[0,15,10],[8,9,4],[3,11,1],[1,3,14],[1,11,3],[9,3,10],[5,1,13],[5,6,14],[1,8,9],[4,7,10],[7,8,15],[12,3,6],[8,12,5],[8,2,14],[3,7,10],[11,9,2],[8,15,2],[0,5,13],[13,0,7],[12,14,11],[4,5,0],[4,7,5],[11,9,6],[13,8,1],[14,1,12],[0,13,8],[14,5,9],[14,5,4],[14,13,12],[5,2,13],[11,14,9],[7,13,4],[15,5,10],[10,9,12],[0,5,3],[11,2,5],[10,6,14],[10,4,0],[3,14,2],[10,7,3],[12,5,4],[14,7,15],[6,1,13],[13,0,8],[12,0,11],[2,11,4],[13,11,0],[6,15,8],[1,12,14],[1,11,5],[9,12,0],[1,11,0],[9,4,2],[10,9,2],[5,12,2],[4,14,8],[9,1,2],[4,7,15],[2,15,5],[0,11,13],[6,0,1],[5,0,13],[15,13,5],[5,0,15],[2,15,11],[2,9,7],[9,5,11],[4,12,2],[12,15,5],[12,14,15],[7,3,14],[2,1,12],[15,1,13],[4,9,0],[9,14,6],[10,15,2],[15,3,12],[10,13,9],[9,7,8],[4,5,7],[13,3,1],[12,0,5],[10,0,9],[13,0,5],[10,7,6],[8,14,6],[4,14,1],[13,1,8],[10,1,4],[9,15,5],[0,1,15],[9,13,2],[15,13,10],[1,7,14],[1,3,13],[9,4,10],[4,0,7],[8,9,6],[9,1,2],[10,1,3],[0,1,4],[5,0,11],[15,0,3],[15,4,1],[2,14,11],[8,9,2],[5,4,8],[4,1,3]],[[9,7,11],[6,4,5],[5,12,8],[13,1,3],[9,5,6],[3,13,1],[0,8,14],[15,14,5],[4,5,2],[3,12,0],[0,7,2],[15,0,2],[11,15,10],[10,13,8],[5,4,2],[13,0,15],[15,4,5],[14,13,4],[10,11,13],[2,12,8],[5,14,0],[8,6,5],[11,15,9],[11,4,12],[2,8,1],[14,8,1],[4,10,15],[3,7,5],[0,10,6],[14,6,15],[2,7,15],[14,1,2],[12,11,8],[4,10,7],[7,8,10],[15,1,2],[4,2,5],[11,10,4],[15,0,8],[6,15,13],[1,2,9],[6,13,15],[11,12,8],[7,6,5],[15,7,2],[10,14,12],[0,10,1],[8,12,7],[1,15,3],[14,8,12],[9,10,3],[8,14,0],[11,8,15],[2,15,13],[8,1,0],[1,7,11],[0,12,1],[4,1,2],[11,1,3],[13,10,14],[11,6,7],[0,7,15],[11,3,5],[15,3,4],[7,11,9],[10,7,9],[5,7,10],[12,7,2],[1,12,10],[6,9,0],[9,8,14],[3,11,1],[4,14,7],[7,8,4],[2,1,3],[8,9,15],[1,2,14],[15,12,0],[14,8,1],[0,11,13],[12,11,4],[11,9,2],[8,4,13],[8,15,3],[0,6,8],[6,9,8],[0,10,6],[3,12,11],[7,10,0],[1,7,5],[6,15,2],[10,7,3],[9,3,7],[12,5,13],[15,5,9],[0,15,8],[6,10,3],[2,14,3],[14,10,13],[12,7,10],[12,0,2],[9,12,15],[4,15,3],[15,4,9],[8,7,13],[15,10,11],[2,11,9],[7,14,13],[5,12,14],[7,14,12],[13,6,0],[5,11,8],[1,7,13],[14,15,4],[11,14,15],[3,1,7],[3,15,0],[9,10,4],[7,14,1],[10,1,13],[1,4,13],[1,4,2],[2,6,15],[0,12,6],[0,7,5],[14,9,8],[11,6,10],[12,8,11],[6,14,1],[10,2,5],[3,13,14],[0,2,9],[14,2,11],[0,11,3],[0,10,7],[1,15,11],[15,0,14],[2,9,12],[5,0,1],[9,4,10],[3,15,0],[15,9,1],[5,14,1],[5,3,15],[3,5,8],[7,3,6],[4,10,14],[13,7,15],[4,9,11],[14,12,1],[6,14,12],[14,11,1],[7,3,0],[9,4,10],[8,9,10],[7,13,4],[9,15,11],[9,7,10],[8,6,7],[10,7,3],[10,13,4],[14,10,11],[13,9,3],[6,8,13],[4,2,9],[0,4,11],[14,13,15],[15,6,14],[9,4,3],[2,12,0],[8,1,2],[4,11,5],[13,2,10],[4,1,11],[1,3,7],[14,13,5],[7,6,14],[8,3,13],[10,2,0],[10,7,1],[13,0,1],[13,1,8],[15,6,10],[15,14,5],[0,5,10],[9,8,1],[15,3,4],[5,4,8],[8,2,11],[11,8,7],[11,14,12],[3,2,8],[11,9,0],[8,2,9],[5,7,1],[15,12,0],[3,10,2],[8,5,10],[5,3,7],[5,11,2],[12,9,4],[3,15,7],[13,10,15],[6,12,8],[1,11,3],[3,5,10],[3,2,11],[5,2,4],[11,10,9],[13,7,15],[4,10,9],[12,5,10],[7,12,14],[6,7,5],[0,8,5],[12,13,15],[13,14,7],[0,3,9],[4,9,12],[2,6,11],[5,14,15],[3,15,8],[14,9,5],[6,5,9],[0,8,9],[13,8,10],[4,15,3],[6,11,4],[12,8,11],[1,11,3],[12,13,11],[1,6,5],[8,6,5],[13,2,0],[15,4,2],[7,12,3],[2,5,6],[15,9,10],[7,8,2],[7,8,3],[0,14,13],[6,1,9],[15,8,6],[5,10,12],[1,15,3],[14,7,9],[3,5,14],[8,15,14],[12,9,13],[5,3,0],[9,11,2],[13,1,2],[6,14,11],[8,7,10],[11,13,14],[15,6,11]],[[0,12,11],[7,14,13],[13,11,7],[9,10,7],[12,0,4],[8,2,6],[0,13,9],[15,10,9],[11,1,0],[12,3,4],[4,1,9],[9,0,15],[12,4,1],[3,7,1],[15,9,0],[12,5,15],[2,0,15],[13,6,1],[8,11,7],[5,15,8],[13,11,1],[5,15,4],[2,13,6],[6,2,7],[10,6,12],[2,13,1],[9,12,10],[14,0,10],[11,6,8],[15,0,2],[1,4,8],[4,9,3],[2,4,11],[0,8,12],[3,1,6],[13,1,4],[8,15,14],[0,7,8],[12,3,9],[11,4,0],[2,5,6],[0,4,8],[10,0,7],[14,5,15],[13,3,2],[10,4,1],[12,14,8],[7,3,2],[15,13,8],[9,0,7],[0,13,12],[3,8,7],[13,7,1],[6,11,9],[0,13,15],[14,3,15],[2,0,9],[14,3,2],[14,11,4],[4,1,8],[12,4,3],[14,6,11],[12,0,13],[10,9,7],[4,1,11],[0,15,3],[3,13,2],[2,6,4],[3,6,1],[12,9,1],[2,7,15],[13,4,12],[12,15,10],[12,14,2],[15,9,6],[14,13,1],[3,6,10],[14,9,5],[11,9,14],[1,13,9],[10,15,5],[7,3,4],[9,2,6],[3,4,8],[15,3,5],[10,5,1],[11,4,5],[7,11,10],[4,9,7],[2,13,4],[2,9,10],[8,15,5],[2,11,9],[10,13,8],[10,1,2],[8,4,3],[7,6,4],[3,14,1],[11,14,15],[6,12,9],[5,13,15],[6,3,7],[8,3,14],[10,15,3],[12,3,13],[3,2,12],[1,10,11],[14,2,3],[3,5,0],[12,4,6],[11,8,9],[0,6,8],[8,1,9],[2,15,8],[10,15,3],[14,0,1],[6,5,2],[1,0,9],[3,11,10],[13,15,9],[2,7,4],[4,2,10],[11,12,1],[0,15,9],[14,2,11],[10,15,2],[5,12,14],[14,7,8],[10,1,3],[0,13,5],[2,8,1],[2,9,6],[6,15,12],[12,7,15],[5,15,3],[15,7,0],[7,3,15],[5,12,9],[7,8,3],[1,9,2],[12,15,0],[3,0,6],[7,5,2],[9,3,4],[11,0,13],[2,8,12],[13,3,10],[8,13,14],[6,5,12],[1,10,5],[2,5,14],[13,6,2],[6,14,9],[6,13,3],[11,2,10],[0,13,5],[8,13,1],[3,15,14],[0,2,15],[6,10,9],[12,1,15],[10,12,15],[12,15,8],[14,13,2],[3,14,5],[8,0,1],[8,5,11],[11,9,5],[14,10,6],[3,1,8],[6,11,12],[5,14,3],[6,9,0],[12,8,15],[3,4,11],[6,10,0],[13,1,10],[8,3,5],[8,4,12],[7,0,10],[13,2,1],[6,14,7],[9,6,11],[1,7,9],[10,12,15],[11,7,0],[0,10,11],[5,0,10],[4,8,11],[3,15,0],[6,8,0],[9,5,0],[3,6,15],[2,6,10],[8,6,3],[4,10,11],[13,14,10],[4,10,15],[12,6,11],[8,12,10],[3,13,2],[5,8,4],[10,6,12],[9,7,13],[0,8,9],[0,13,3],[6,13,5],[2,14,11],[14,6,1],[9,12,10],[10,1,6],[15,6,8],[13,6,11],[2,11,13],[10,8,5],[10,0,11],[12,9,0],[11,8,9],[13,15,0],[2,14,0],[9,11,0],[5,11,0],[10,6,5],[3,14,12],[14,1,0],[0,14,6],[6,14,5],[6,15,11],[13,10,5],[12,0,9],[6,13,3],[11,1,15],[6,15,14],[12,14,15],[15,5,11],[1,4,13],[12,1,8],[15,3,9],[9,2,11],[6,8,10],[12,9,15],[8,0,4],[1,11,9],[15,10,13],[6,5,9],[6,1,8],[13,14,7],[10,4,13],[6,0,7],[4,5,8],[15,7,1],[4,9,12],[8,7,1],[5,3,11],[7,5,2],[15,1,3]],[[4,10,5],[7,5,0],[3,5,14],[1,8,14],[2,14,12],[0,8,14],[7,12,8],[14,10,0],[3,11,13],[6,13,9],[10,12,11],[13,2,0],[11,4,15],[1,12,10],[12,2,15],[11,13,10],[15,9,14],[15,3,8],[10,6,3],[11,4,2],[15,3,2],[4,1,14],[4,2,7],[9,1,12],[8,0,14],[10,12,6],[14,10,1],[2,12,7],[13,10,9],[0,11,12],[0,10,1],[1,15,9],[4,13,2],[5,13,2],[11,2,0],[8,5,3],[8,9,11],[5,12,14],[5,1,12],[1,6,11],[10,1,0],[5,11,4],[12,7,2],[12,13,11],[10,15,13],[12,4,15],[9,6,11],[5,10,3],[3,7,1],[13,8,4],[4,9,6],[2,4,8],[15,9,1],[4,0,10],[3,2,7],[0,10,11],[11,4,8],[14,3,10],[10,13,4],[0,14,6],[14,9,2],[13,5,0],[2,7,6],[0,13,14],[5,10,11],[5,13,2],[14,8,6],[13,3,2],[6,11,3],[9,4,1],[7,2,10],[8,11,2],[9,5,4],[14,2,4],[5,14,4],[10,13,2],[12,4,1],[11,3,6],[6,11,14],[5,12,4],[12,9,7],[9,12,1],[5,10,3],[12,13,11],[11,1,2],[2,13,12],[14,13,2],[1,11,10],[13,15,1],[0,2,13],[10,5,9],[3,12,2],[11,3,5],[1,10,12],[10,3,4],[11,1,7],[15,5,2],[5,0,14],[7,8,0],[14,5,15],[4,8,12],[11,9,7],[1,12,8],[0,8,4],[5,4,6],[5,11,1],[5,3,7],[5,6,14],[6,14,2],[10,8,7],[2,5,6],[15,13,1],[12,4,13],[15,2,4],[8,11,12],[10,5,2],[11,13,8],[8,5,11],[9,12,10],[0,7,15],[11,1,0],[8,4,3],[7,5,14],[0,13,1],[7,6,11],[0,3,8],[12,3,1],[2,12,13],[4,12,0],[15,9,11],[2,6,13],[15,0,12],[2,8,10],[11,14,3],[4,15,2],[3,5,11],[6,14,9],[7,4,1],[7,9,13],[4,7,10],[0,4,9],[15,0,8],[13,2,11],[7,13,11],[0,12,11],[8,9,11],[7,15,6],[7,4,11],[12,0,3],[2,4,7],[5,12,9],[5,9,10],[5,2,9],[9,5,3],[6,1,2],[6,5,0],[7,14,8],[13,1,9],[8,9,12],[1,15,4],[11,9,6],[0,3,10],[14,11,3],[9,15,6],[0,14,11],[0,8,11],[9,11,15],[13,5,15],[12,0,9],[1,7,15],[8,0,3],[10,3,8],[11,1,14],[1,5,7],[11,7,15],[5,11,7],[5,6,14],[13,5,7],[11,1,6],[14,10,4],[12,11,6],[14,1,7],[5,10,3],[3,0,5],[12,0,13],[1,5,0],[13,4,7],[9,14,10],[6,11,7],[13,0,7],[4,2,3],[13,11,10],[5,12,7],[11,10,7],[1,14,9],[12,13,11],[13,7,14],[7,15,12],[9,4,12],[4,10,11],[12,6,14],[6,2,14],[2,14,1],[2,11,15],[13,5,9],[15,1,12],[6,7,14],[2,4,13],[12,8,1],[5,3,6],[14,4,13],[2,11,5],[4,1,12],[4,12,6],[1,5,13],[12,15,1],[4,2,3],[10,3,12],[4,14,9],[9,15,1],[11,5,4],[5,15,2],[5,1,11],[9,13,4],[15,2,8],[3,7,8],[9,8,10],[11,15,8],[7,4,12],[8,1,2],[3,2,5],[1,6,8],[9,13,14],[3,13,15],[15,4,6],[0,10,5],[0,14,5],[5,9,2],[3,4,14],[7,5,0],[10,7,12],[13,8,14],[15,8,11],[7,1,15],[9,15,4],[3,11,0],[12,7,14],[3,12,13],[8,2,5],[15,6,7],[4,10,15],[12,8,13],[1,13,9],[15,9,11],[2,8,6],[13,7,11]],[[3,10,4],[2,15,13],[5,8,15],[8,10,13],[7,2,3],[2,12,9],[4,8,15],[6,12,5],[13,2,8],[3,15,13],[9,2,1],[13,3,9],[0,11,1],[8,3,1],[10,3,5],[11,7,4],[0,2,15],[14,8,10],[7,6,14],[2,3,15],[1,0,5],[6,2,11],[9,11,6],[9,1,3],[3,15,13],[0,9,3],[14,2,9],[12,3,10],[1,10,6],[15,2,10],[5,15,11],[10,6,4],[4,12,8],[14,7,1],[3,0,5],[12,13,1],[3,8,4],[2,7,14],[4,14,7],[6,2,0],[8,15,3],[3,5,7],[9,14,2],[8,2,1],[13,7,1],[7,5,14],[1,2,7],[2,9,13],[5,12,13],[6,11,15],[13,1,3],[7,13,8],[4,3,1],[14,9,12],[3,8,0],[13,7,2],[1,2,10],[5,15,13],[11,3,4],[10,14,8],[0,11,13],[6,3,0],[2,15,7],[10,7,0],[15,3,14],[1,3,14],[11,3,13],[1,7,5],[6,4,9],[4,3,10],[14,11,5],[9,2,4],[2,15,7],[5,2,8],[0,6,4],[8,4,5],[15,12,8],[8,5,12],[13,1,4],[11,7,15],[9,11,8],[1,9,6],[9,11,10],[14,9,6],[12,5,2],[8,3,12],[6,12,5],[1,9,0],[11,10,13],[13,14,0],[1,11,0],[14,11,9],[0,11,14],[5,0,12],[4,0,2],[15,9,3],[3,10,13],[13,1,3],[13,0,1],[1,8,9],[10,1,9],[14,0,10],[3,5,12],[13,11,8],[0,12,2],[15,4,1],[5,7,11],[12,3,6],[12,2,4],[10,6,0],[12,15,4],[5,6,10],[5,6,0],[11,0,1],[5,6,0],[12,6,14],[3,0,11],[12,10,9],[13,10,8],[12,8,11],[12,8,14],[8,12,14],[6,8,11],[12,13,1],[13,8,9],[10,14,8],[2,12,8],[0,4,9],[6,1,8],[10,14,6],[6,3,0],[15,2,14],[11,3,6],[1,8,0],[7,14,13],[4,8,3],[14,11,0],[15,4,14],[9,12,10],[6,12,13],[12,1,13],[4,5,8],[8,14,11],[6,11,1],[8,1,4],[10,9,14],[1,10,12],[5,11,3],[14,12,3],[10,4,6],[3,8,6],[10,1,3],[13,12,15],[14,13,7],[11,9,4],[15,5,4],[14,9,0],[0,4,3],[14,12,5],[9,0,14],[12,3,8],[13,3,11],[9,3,5],[1,8,13],[15,2,1],[2,6,7],[3,11,2],[12,14,3],[11,1,8],[1,2,14],[14,6,8],[13,7,3],[12,15,3],[0,7,13],[4,8,7],[7,1,5],[7,15,12],[12,14,7],[7,8,4],[9,1,12],[7,4,13],[14,2,4],[10,15,8],[9,11,5],[2,0,6],[11,12,6],[11,15,8],[8,10,1],[7,9,15],[6,5,0],[11,14,0],[5,3,10],[1,6,2],[7,10,6],[11,7,1],[10,1,14],[12,1,5],[3,15,12],[7,2,15],[1,2,13],[15,7,11],[5,6,3],[4,1,7],[15,11,12],[2,12,5],[11,12,10],[7,4,6],[6,1,7],[3,0,5],[3,0,8],[12,4,0],[2,7,12],[8,7,14],[2,5,7],[11,12,9],[1,11,12],[3,7,1],[3,10,12],[10,0,7],[5,7,8],[14,0,10],[9,11,6],[1,8,14],[14,6,9],[3,5,15],[14,1,13],[0,1,2],[5,9,1],[5,10,1],[2,0,10],[15,2,3],[0,11,5],[14,15,13],[4,9,0],[14,13,10],[6,4,5],[3,6,15],[5,7,6],[10,15,6],[8,4,10],[2,14,15],[3,10,2],[5,9,0],[8,11,0],[3,15,14],[7,1,12],[3,12,15],[8,9,5],[14,13,6],[1,8,12],[4,7,9],[7,8,1],[5,6,14],[12,4,3],[1,2,6],[13,8,7]],[[14,4,7],[4,3,14],[7,8,1],[11,8,14],[9,13,1],[1,8,7],[15,0,4],[14,8,4],[15,2,3],[2,14,0],[0,7,4],[13,12,11],[14,15,4],[9,10,4],[4,2,9],[13,4,3],[14,4,10],[2,4,12],[8,9,5],[11,4,13],[6,0,1],[4,7,0],[4,6,3],[15,13,2],[7,3,5],[8,2,13],[4,0,13],[10,9,7],[8,4,14],[5,9,11],[5,4,10],[5,4,8],[11,13,14],[9,10,13],[2,6,8],[2,8,15],[3,11,12],[12,0,4],[8,14,5],[10,0,12],[8,2,3],[5,2,14],[15,10,3],[4,12,7],[12,11,5],[4,6,7],[10,1,2],[12,5,8],[10,8,6],[6,3,8],[15,4,0],[10,13,0],[1,4,2],[14,13,2],[14,10,13],[12,13,10],[14,13,15],[1,12,6],[8,6,3],[7,3,5],[1,7,10],[3,5,2],[3,10,9],[1,11,2],[5,12,1],[7,9,10],[8,7,4],[9,1,8],[4,7,6],[8,7,1],[11,1,5],[5,12,7],[9,14,1],[0,15,8],[7,3,6],[15,7,11],[3,1,2],[10,13,0],[3,0,10],[3,9,10],[14,8,0],[5,1,12],[4,3,13],[7,15,2],[5,6,9],[5,6,2],[8,7,11],[5,8,1],[9,6,3],[0,5,10],[3,10,12],[13,6,8],[11,3,5],[14,3,11],[3,13,0],[2,11,7],[5,14,9],[11,1,0],[8,7,0],[6,3,10],[6,11,10],[13,8,3],[0,13,9],[8,4,0],[6,14,3],[7,1,5],[10,14,12],[5,8,15],[0,14,9],[11,7,12],[5,10,14],[0,12,11],[14,3,13],[15,11,6],[2,4,5],[4,11,3],[12,9,11],[6,4,1],[3,9,0],[15,11,6],[15,1,4],[12,9,7],[6,14,0],[5,3,8],[3,0,15],[5,9,0],[13,7,11],[14,13,0],[2,13,14],[6,1,2],[0,13,15],[13,15,0],[13,9,11],[5,15,11],[1,2,3],[2,0,12],[15,10,9],[9,10,13],[6,11,9],[4,10,13],[9,1,10],[6,8,13],[6,8,3],[7,14,12],[8,13,1],[8,4,10],[1,3,12],[2,3,7],[5,0,1],[9,0,2],[10,5,14],[10,12,7],[9,3,10],[2,0,14],[2,5,11],[11,14,0],[13,14,10],[10,11,1],[11,2,13],[6,14,8],[8,11,5],[1,12,9],[11,0,8],[5,6,12],[15,13,3],[9,0,4],[14,2,13],[3,2,10],[15,8,0],[14,4,0],[10,3,14],[8,1,9],[10,0,11],[9,3,8],[12,4,7],[6,15,1],[12,7,5],[11,0,9],[4,12,5],[8,1,10],[2,0,1],[4,12,10],[11,15,8],[0,14,10],[14,13,6],[3,12,1],[7,11,2],[8,15,7],[11,10,15],[5,9,6],[5,6,11],[7,15,1],[9,0,11],[2,8,9],[1,15,3],[3,2,8],[13,0,4],[9,7,4],[6,1,7],[3,0,13],[8,5,6],[10,1,8],[8,10,12],[8,0,15],[15,12,5],[15,10,4],[15,1,5],[7,1,14],[4,7,3],[3,1,14],[14,9,3],[0,8,1],[8,12,9],[5,12,2],[3,9,7],[6,2,13],[15,10,7],[2,6,5],[8,1,15],[2,10,8],[7,10,9],[5,10,1],[15,4,0],[4,13,0],[3,13,9],[13,7,5],[9,13,1],[4,14,12],[4,3,13],[14,11,5],[3,8,0],[12,15,11],[9,10,12],[14,2,8],[9,12,8],[10,13,12],[13,0,3],[7,5,10],[2,11,7],[3,13,2],[8,10,5],[5,0,3],[8,4,13],[10,3,8],[13,12,8],[0,13,12],[7,14,9],[10,0,6],[3,5,10],[11,7,8],[6,1,13],[15,6,8],[2,14,15],[12,4,9],[7,9,5],[12,5,2]],[[3,0,5],[11,7,3],[4,14,9],[0,13,15],[2,15,8],[3,0,4],[1,5,12],[9,8,14],[13,6,4],[7,6,0],[9,15,0],[14,6,15],[3,9,10],[2,12,9],[12,7,14],[6,8,1],[0,5,9],[2,1,9],[14,12,6],[11,8,3],[7,6,14],[6,11,13],[5,1,3],[12,6,7],[8,13,1],[0,7,15],[10,7,15],[8,10,6],[6,15,12],[13,9,3],[4,10,2],[13,4,3],[14,8,15],[7,2,11],[1,7,13],[11,4,5],[2,11,1],[9,10,14],[12,13,10],[12,8,7],[4,12,15],[4,14,11],[12,5,7],[0,4,9],[3,5,7],[0,13,6],[4,14,2],[2,10,14],[11,12,13],[11,0,3],[5,6,8],[9,1,15],[8,6,12],[11,15,6],[12,15,7],[10,4,6],[6,5,9],[9,14,7],[3,14,8],[1,15,14],[4,10,3],[13,4,6],[12,3,9],[6,1,12],[1,0,13],[8,15,11],[3,15,5],[6,8,11],[5,0,14],[9,3,15],[0,14,9],[2,8,15],[5,8,12],[15,14,3],[6,8,15],[15,1,0],[1,12,13],[2,13,12],[14,7,10],[15,2,1],[3,7,14],[7,10,5],[13,10,4],[5,3,6],[9,14,13],[5,10,6],[8,3,9],[2,6,8],[15,7,9],[11,8,6],[10,3,2],[14,1,4],[5,13,14],[15,14,7],[3,14,8],[0,14,4],[0,6,10],[10,2,11],[14,12,7],[12,1,14],[9,14,10],[2,3,8],[14,4,1],[7,2,14],[15,7,6],[13,3,8],[7,2,3],[8,11,13],[2,9,14],[6,7,1],[4,1,2],[13,2,12],[15,4,11],[7,4,3],[8,6,13],[9,7,2],[2,1,13],[9,6,7],[3,6,12],[6,3,13],[0,13,8],[1,9,13],[8,13,9],[0,13,6],[0,6,14],[2,4,12],[15,1,2],[3,11,14],[5,4,15],[7,9,4],[10,4,15],[9,2,6],[10,6,2],[14,13,7],[0,15,4],[5,4,13],[11,0,14],[4,11,6],[10,11,5],[0,15,5],[2,11,10],[0,4,11],[4,12,8],[5,4,8],[15,13,3],[9,7,6],[4,3,9],[13,6,12],[6,1,3],[11,3,13],[6,9,12],[9,5,4],[8,3,6],[4,15,0],[15,5,11],[13,7,14],[8,15,12],[11,12,3],[15,5,9],[1,5,10],[7,14,0],[5,1,3],[9,0,2],[5,14,1],[15,9,2],[8,1,6],[6,8,14],[13,12,7],[11,2,5],[6,1,11],[1,3,2],[4,12,14],[6,2,4],[5,9,12],[4,7,14],[12,1,4],[8,5,1],[10,12,3],[15,4,3],[3,11,6],[3,4,11],[12,6,2],[4,1,11],[5,4,15],[8,15,9],[4,14,12],[4,9,5],[12,11,2],[15,10,9],[2,7,10],[7,4,0],[11,0,2],[0,11,6],[11,9,14],[7,11,12],[4,5,2],[4,8,9],[8,11,7],[11,0,1],[12,5,1],[1,0,5],[11,15,6],[10,15,6],[9,8,15],[5,10,13],[15,6,0],[13,9,7],[12,1,2],[4,7,13],[5,6,15],[15,8,10],[1,3,9],[6,14,11],[8,12,0],[9,8,2],[13,6,3],[12,7,13],[2,9,5],[5,9,3],[7,3,5],[5,13,6],[1,9,12],[9,15,3],[5,2,14],[6,0,7],[11,15,3],[5,14,10],[2,4,13],[13,10,0],[5,15,13],[6,2,3],[5,15,13],[15,5,8],[2,13,11],[5,13,14],[14,7,10],[5,12,1],[10,13,4],[3,13,10],[10,15,4],[2,5,13],[2,7,6],[14,15,0],[2,7,0],[14,6,4],[0,15,13],[12,4,0],[15,1,10],[6,14,11],[8,5,13],[0,12,5],[0,13,6],[12,8,1],[2,0,4],[6,14,10],[7,15,11]],[[3,0,10],[14,3,11],[6,3,1],[7,5,2],[6,5,10],[8,10,14],[1,9,2],[8,2,10],[6,0,10],[13,12,11],[0,13,10],[0,9,2],[13,3,11],[0,6,4],[5,9,2],[9,12,7],[12,3,15],[14,1,4],[3,1,15],[11,14,6],[5,10,0],[2,5,11],[11,13,12],[10,9,5],[8,5,13],[4,7,11],[2,4,15],[15,2,7],[0,10,15],[14,5,9],[15,4,9],[9,14,13],[8,12,15],[2,3,5],[11,1,10],[3,4,9],[4,0,9],[12,7,2],[3,4,15],[13,9,5],[15,0,1],[0,4,2],[7,12,5],[7,10,8],[14,9,3],[7,0,2],[4,14,11],[13,3,0],[1,8,12],[9,0,7],[0,4,2],[3,10,5],[12,15,3],[12,5,3],[13,9,14],[15,11,4],[14,7,9],[5,7,1],[10,13,5],[8,11,14],[12,0,4],[10,3,14],[3,4,11],[15,1,5],[12,2,9],[0,1,14],[15,5,7],[3,0,14],[11,6,13],[9,0,10],[13,7,6],[10,8,15],[14,0,6],[13,1,0],[3,2,9],[9,8,12],[1,11,14],[3,12,13],[1,13,12],[5,2,1],[12,6,1],[1,11,9],[8,2,4],[10,9,11],[2,5,1],[14,5,9],[6,3,2],[0,4,1],[4,6,7],[5,4,2],[14,6,15],[0,12,14],[12,9,3],[8,3,13],[8,9,11],[6,15,10],[0,5,10],[8,0,12],[9,13,5],[0,5,12],[3,2,8],[0,1,3],[14,0,5],[14,3,0],[9,3,0],[12,5,11],[14,13,7],[12,6,9],[11,0,10],[8,0,10],[7,14,4],[1,6,12],[9,4,0],[7,1,2],[3,10,4],[7,14,0],[13,7,12],[3,13,6],[13,14,11],[12,7,5],[6,14,2],[15,1,2],[10,1,8],[8,10,13],[8,12,7],[0,12,10],[2,9,12],[6,10,4],[2,4,14],[10,14,9],[15,0,8],[15,0,9],[13,8,12],[2,1,15],[6,9,4],[0,9,12],[3,13,0],[2,0,5],[2,0,15],[1,4,6],[9,14,3],[10,3,1],[8,13,11],[1,6,8],[8,3,13],[3,7,4],[13,11,9],[1,8,12],[0,3,1],[5,7,4],[10,6,9],[11,1,14],[15,14,0],[3,13,8],[2,5,0],[13,0,7],[12,15,11],[7,13,9],[1,4,9],[15,14,2],[11,10,8],[12,1,8],[3,15,6],[10,1,12],[10,12,4],[15,8,10],[9,13,8],[11,8,7],[6,5,12],[6,1,10],[11,0,12],[5,15,9],[9,4,0],[6,15,8],[1,8,5],[2,8,1],[0,3,6],[5,12,2],[13,6,5],[1,15,14],[4,1,9],[3,6,8],[6,12,10],[5,0,2],[15,8,6],[13,10,9],[2,0,15],[7,11,0],[12,9,3],[14,9,7],[14,12,4],[6,3,0],[15,14,5],[10,5,7],[14,0,10],[12,9,0],[0,11,4],[15,3,7],[0,6,11],[10,3,7],[15,2,8],[3,8,2],[3,14,0],[2,0,11],[1,6,15],[15,10,0],[14,2,9],[8,6,10],[15,3,0],[13,9,2],[10,4,9],[6,0,5],[1,7,12],[1,8,0],[12,13,2],[2,9,7],[13,5,10],[4,14,9],[5,8,12],[4,13,1],[0,3,4],[8,7,1],[5,6,3],[9,1,8],[11,6,3],[1,0,9],[13,0,14],[3,9,11],[14,1,15],[7,3,0],[13,10,15],[14,11,12],[3,7,14],[9,15,11],[15,0,3],[9,14,10],[10,12,8],[11,5,10],[2,11,14],[9,12,15],[6,7,10],[2,4,13],[4,8,10],[10,5,6],[4,15,0],[8,0,6],[8,13,6],[3,1,2],[2,9,1],[9,13,4],[1,3,8],[7,3,11],[13,1,11],[14,3,12],[1,4,9],[1,13,15]]]
ZW = 806
def setup_inputs(rng):
    return {"z": rng.standard_normal((N, 128, ZW), dtype=np.float32)}
def reference(z):
    y = np.zeros((N, 128, T), np.float64)
    fill = [0] * N
    for r in range(N):
        for t in range(T):
            for e in ROUTE[r][t]:
                y[r][:, t] += z[e][:, fill[e]].astype(np.float64)
                fill[e] += 1
    return {"y": y.astype(z.dtype)}

@@ -1,0 +1,104 @@
+from concourse.bass import DstId, RemoteDMATransfer
+
+SCRATCH = {
+    "zs": ("sbuf", [128, 806], "float32"),
+    "land": ("sbuf", [128, 704], "float32"),
+    "acc": ("sbuf", [128, 256], "float32"),
+}
+SEMAPHORES = ["loaded", "stored", "arrived", "sent", "done"]
+
+PLAN = {}
+
+
+def engines(mask):
+    return bin(mask).count("1")
+
+
+def make_plan(T, topo):
+    route, cores = T.tables["ROUTE"], list(T.cores)
+    n, nt = len(cores), len(route[0])
+    par = [topo.chip(c) & 1 for c in cores]
+    folder, agg = [], []
+    for c in cores:
+        b, k = topo.chip(c), c % 8
+        folder.append(8 * b + (1 if k == 3 else 5))
+        agg.append(8 * (b ^ 1) + (2 if k == 3 else 6))
+    fill = [0] * n
+    sends = [[] for _ in range(n)]
+    role = {}
+    for r in range(n):
+        off = list(fill)
+        where = [[] for _ in range(nt)]
+        for t in range(nt):
+            for e in route[r][t]:
+                where[t].append((e, fill[e]))
+                fill[e] += 1
+        base, top, expect = [0] * n, {0: 0, 1: 0}, {0: 0, 1: 0}
+        for e in range(n):
+            far = int(par[e] != par[r])
+            w = fill[e] - off[e]
+            base[e] = top[far]
+            top[far] += w
+            if w:
+                dst = agg[r] if far else folder[r]
+                sends[e].append((dst, off[e], base[e], w))
+                expect[far] += engines(topo.mask(cores[e], dst))
+        fjobs, ajobs = [], []
+        for t in range(nt):
+            near = [base[e] + c - off[e] for e, c in where[t] if par[e] == par[r]]
+            far = [base[e] + c - off[e] for e, c in where[t] if par[e] != par[r]]
+            if far and near:
+                ajobs.append((far, folder[r], "land", top[0], "arrived"))
+                near.append(top[0])
+                top[0] += 1
+                expect[0] += 1
+            elif far:
+                ajobs.append((far, cores[r], "acc", t, "done"))
+            if near:
+                fjobs.append((near, cores[r], "acc", t, "done"))
+        role[folder[r]] = (expect[0], fjobs)
+        role[agg[r]] = (expect[1], ajobs)
+    return {"sends": sends, "role": role, "nt": nt}
+
+
+def rank_program(g, core, T, topo):
+    if "p" not in PLAN:
+        PLAN["p"] = make_plan(T, topo)
+    plan = PLAN["p"]
+    rank = T.rank_of(core)
+
+    if rank is not None:
+        g.dma_start(T.zs[:], T.z[:]).then_inc(T.sem.loaded, 16)
+        g.wait_ge(T.sem.loaded, 16)
+        sent = 0
+        for dst, zo, lo, w in plan["sends"][rank]:
+            rid, pid, _ = topo.addr(dst)
+            m = topo.mask(core, dst)
+            g.remote_dma(T.land[:, lo:lo + w], T.zs[:, zo:zo + w], T.sem.arrived, T.sem.sent, pid, rid, m)
+            sent += engines(m)
+        g.wait_ge(T.sem.done, plan["nt"])
+        g.dma_start(T.y[:], T.acc[:]).then_inc(T.sem.stored, 16)
+        g.wait_ge(T.sem.stored, 16)
+        g.wait_ge(T.sem.sent, sent)
+        return
+
+    if core not in plan["role"]:
+        return
+    expect, jobs = plan["role"][core]
+    g.wait_ge(T.sem.arrived, expect)
+    sent = 0
+    for nsrc in (1, 2, 3):
+        some = [j for j in jobs if len(j[0]) == nsrc]
+        while some:
+            width = engines(topo.mask(core, some[0][1]))
+            batch, some = some[:width], some[width:]
+            trs = []
+            for i, (srcs, dst, buf, col, sem) in enumerate(batch):
+                rid, pid, _ = topo.addr(dst)
+                aps = [T.land[:, c:c + 1] for c in srcs]
+                trs.append(RemoteDMATransfer(dst_ids=[DstId(rid=rid, pnc=pid)], dma_engine_mask=1 << i,
+                                             remote_sem=T.sem[sem], srcs=aps, dsts=[T[buf][:, col:col + 1]],
+                                             alu_op=1 if nsrc > 1 else 0))
+            g.remote_dma_fused(trs, local_sem=T.sem.sent)
+            sent += len(trs)
+    g.wait_ge(T.sem.sent, sent)

@@ -1,11 +1,16 @@
 from concourse.bass import DstId, RemoteDMATransfer
+from concourse.mybir import AluOpType
 
 SCRATCH = {
     "zs": ("sbuf", [128, 806], "float32"),
-    "land": ("sbuf", [128, 704], "float32"),
-    "acc": ("sbuf", [128, 256], "float32"),
+    "land": ("sbuf", [128, 320], "float32"),
+    "S": ("sbuf", [128, 256], "float32"),
+    "M": ("sbuf", [128, 256], "float32"),
 }
-SEMAPHORES = ["loaded", "stored", "arrived", "sent", "done"]
+SEMAPHORES = ["loaded", "added", "stored", "arrived", "sent", "done"]
+
+FOLDERS = {3: ((4, 0.32), (5, 0.56), (1, 0.12)), 4: ((1, 0.44), (0, 0.56))}
+AGGREGATORS = {3: ((3, 0.37), (2, 0.63)), 4: ((6, 0.5), (7, 0.5))}
 
 PLAN = {}
 
@@ -14,51 +19,91 @@ def engines(mask):
     return bin(mask).count("1")
 
 
+def split(weights, shares):
+    total, owner, run, k = sum(weights), [], 0, 0
+    goal = shares[0] * total
+    for w in weights:
+        while k + 1 < len(shares) and run + w / 2.0 > goal:
+            k += 1
+            goal += shares[k] * total
+        owner.append(k)
+        run += w
+    return owner
+
+
 def make_plan(T, topo):
     route, cores = T.tables["ROUTE"], list(T.cores)
     n, nt = len(cores), len(route[0])
     par = [topo.chip(c) & 1 for c in cores]
-    folder, agg = [], []
-    for c in cores:
-        b, k = topo.chip(c), c % 8
-        folder.append(8 * b + (1 if k == 3 else 5))
-        agg.append(8 * (b ^ 1) + (2 if k == 3 else 6))
     fill = [0] * n
-    sends = [[] for _ in range(n)]
-    role = {}
+    tokens = []
     for r in range(n):
-        off = list(fill)
-        where = [[] for _ in range(nt)]
+        b, k = topo.chip(cores[r]), cores[r] % 8
+        rows = []
         for t in range(nt):
+            near, far = [], []
             for e in route[r][t]:
-                where[t].append((e, fill[e]))
+                (near if par[e] == par[r] else far).append((e, fill[e]))
                 fill[e] += 1
-        base, top, expect = [0] * n, {0: 0, 1: 0}, {0: 0, 1: 0}
-        for e in range(n):
-            far = int(par[e] != par[r])
-            w = fill[e] - off[e]
-            base[e] = top[far]
-            top[far] += w
-            if w:
-                dst = agg[r] if far else folder[r]
-                sends[e].append((dst, off[e], base[e], w))
-                expect[far] += engines(topo.mask(cores[e], dst))
-        fjobs, ajobs = [], []
+            rows.append((near, far))
+        fo = split([(2 if not f else 1) if nr else 0 for nr, f in rows], [s for _, s in FOLDERS[k]])
+        ao = split([1 if f else 0 for nr, f in rows], [s for _, s in AGGREGATORS[k]])
         for t in range(nt):
-            near = [base[e] + c - off[e] for e, c in where[t] if par[e] == par[r]]
-            far = [base[e] + c - off[e] for e, c in where[t] if par[e] != par[r]]
-            if far and near:
-                ajobs.append((far, folder[r], "land", top[0], "arrived"))
-                near.append(top[0])
-                top[0] += 1
-                expect[0] += 1
-            elif far:
-                ajobs.append((far, cores[r], "acc", t, "done"))
-            if near:
-                fjobs.append((near, cores[r], "acc", t, "done"))
-        role[folder[r]] = (expect[0], fjobs)
-        role[agg[r]] = (expect[1], ajobs)
-    return {"sends": sends, "role": role, "nt": nt}
+            tokens.append((r, t, rows[t][0], rows[t][1], 8 * b + FOLDERS[k][fo[t]][0],
+                           8 * (b ^ 1) + AGGREGATORS[k][ao[t]][0]))
+    pieces = {}
+    for r, t, near, far, fc, ac in tokens:
+        for group, h in ((near, fc), (far, ac)):
+            for e, c in group:
+                if cores[e] == h:
+                    continue
+                lst = pieces.setdefault((h, e), [])
+                if lst and lst[-1][1] == c:
+                    lst[-1][1] = c + 1
+                else:
+                    lst.append([c, c + 1])
+    top, expect, place = {}, {}, {}
+    sends = [[] for _ in range(n)]
+    for h, e in sorted(pieces):
+        for lo, hi in pieces[(h, e)]:
+            at = top.get(h, 0)
+            top[h] = at + hi - lo
+            sends[e].append((h, lo, at, hi - lo))
+            expect[h] = expect.get(h, 0) + engines(topo.mask(cores[e], h))
+            for c in range(lo, hi):
+                place[(h, e, c)] = at + c - lo
+    assert max(top.values()) <= SCRATCH["land"][1][1]
+
+    def src(h, group):
+        return [("zs", c) if cores[e] == h else ("land", place[(h, e, c)]) for e, c in group]
+
+    jobs = {}
+    done, has_m = [0] * n, [[False] * nt for _ in range(n)]
+    for r, t, near, far, fc, ac in tokens:
+        if not far:
+            out = [(fc, near[:2], "S"), (fc, near[2:], "M")]
+        elif not near:
+            out = [(ac, far, "S")]
+        else:
+            out = [(fc, near, "S"), (ac, far, "M")]
+        for h, group, buf in out:
+            jobs.setdefault(h, []).append((src(h, group), cores[r], buf, t))
+            done[r] += 1
+            if buf == "M":
+                has_m[r][t] = True
+    runs = []
+    for r in range(n):
+        rr, t = [], 0
+        while t < nt:
+            if has_m[r][t]:
+                a = t
+                while t < nt and has_m[r][t]:
+                    t += 1
+                rr.append((a, t))
+            else:
+                t += 1
+        runs.append(rr)
+    return {"sends": sends, "jobs": jobs, "expect": expect, "done": done, "runs": runs}
 
 
 def rank_program(g, core, T, topo):
@@ -66,39 +111,40 @@ def rank_program(g, core, T, topo):
         PLAN["p"] = make_plan(T, topo)
     plan = PLAN["p"]
     rank = T.rank_of(core)
+    sent = 0
 
     if rank is not None:
         g.dma_start(T.zs[:], T.z[:]).then_inc(T.sem.loaded, 16)
         g.wait_ge(T.sem.loaded, 16)
-        sent = 0
         for dst, zo, lo, w in plan["sends"][rank]:
             rid, pid, _ = topo.addr(dst)
             m = topo.mask(core, dst)
             g.remote_dma(T.land[:, lo:lo + w], T.zs[:, zo:zo + w], T.sem.arrived, T.sem.sent, pid, rid, m)
             sent += engines(m)
-        g.wait_ge(T.sem.done, plan["nt"])
-        g.dma_start(T.y[:], T.acc[:]).then_inc(T.sem.stored, 16)
-        g.wait_ge(T.sem.stored, 16)
-        g.wait_ge(T.sem.sent, sent)
-        return
 
-    if core not in plan["role"]:
-        return
-    expect, jobs = plan["role"][core]
-    g.wait_ge(T.sem.arrived, expect)
-    sent = 0
-    for nsrc in (1, 2, 3):
-        some = [j for j in jobs if len(j[0]) == nsrc]
-        while some:
-            width = engines(topo.mask(core, some[0][1]))
-            batch, some = some[:width], some[width:]
-            trs = []
-            for i, (srcs, dst, buf, col, sem) in enumerate(batch):
-                rid, pid, _ = topo.addr(dst)
-                aps = [T.land[:, c:c + 1] for c in srcs]
-                trs.append(RemoteDMATransfer(dst_ids=[DstId(rid=rid, pnc=pid)], dma_engine_mask=1 << i,
-                                             remote_sem=T.sem[sem], srcs=aps, dsts=[T[buf][:, col:col + 1]],
-                                             alu_op=1 if nsrc > 1 else 0))
-            g.remote_dma_fused(trs, local_sem=T.sem.sent)
-            sent += len(trs)
-    g.wait_ge(T.sem.sent, sent)
+    if core in plan["jobs"]:
+        g.wait_ge(T.sem.arrived, plan["expect"][core])
+        width = min(engines(topo.mask(core, j[1])) for j in plan["jobs"][core])
+        for nsrc in (1, 2, 3):
+            some = [j for j in plan["jobs"][core] if len(j[0]) == nsrc]
+            while some:
+                batch, some = some[:width], some[width:]
+                trs = []
+                for i, (srcs, dst, buf, col) in enumerate(batch):
+                    rid, pid, _ = topo.addr(dst)
+                    trs.append(RemoteDMATransfer(dst_ids=[DstId(rid=rid, pnc=pid)], dma_engine_mask=1 << i,
+                                                 remote_sem=T.sem.done, srcs=[T[b][:, c:c + 1] for b, c in srcs],
+                                                 dsts=[T[buf][:, col:col + 1]], alu_op=1 if nsrc > 1 else 0))
+                g.remote_dma_fused(trs, local_sem=T.sem.sent)
+                sent += len(trs)
+
+    if rank is not None:
+        g.wait_ge(T.sem.done, plan["done"][rank])
+        for a, b in plan["runs"][rank]:
+            g.dma_start(T.S[:, a:b], T.M[:, a:b], accum_op=AluOpType.add).then_inc(T.sem.added, 16)
+        g.wait_ge(T.sem.added, 16 * len(plan["runs"][rank]))
+        g.dma_start(T.y[:], T.S[:]).then_inc(T.sem.stored, 16)
+        g.wait_ge(T.sem.stored, 16)
+
+    if sent:
+        g.wait_ge(T.sem.sent, sent)

from concourse.bass import DstId, RemoteDMATransfer
from concourse.mybir import AluOpType

SCRATCH = {
    "zs": ("sbuf", [128, 806], "float32"),
    "land": ("sbuf", [128, 320], "float32"),
    "S": ("sbuf", [128, 256], "float32"),
    "M": ("sbuf", [128, 256], "float32"),
}
SEMAPHORES = ["loaded", "added", "stored", "arrived", "sent", "done"]

FOLDERS = {3: ((4, 0.32), (5, 0.56), (1, 0.12)), 4: ((1, 0.44), (0, 0.56))}
AGGREGATORS = {3: ((3, 0.37), (2, 0.63)), 4: ((6, 0.5), (7, 0.5))}

PLAN = {}


def engines(mask):
    return bin(mask).count("1")


def split(weights, shares):
    total, owner, run, k = sum(weights), [], 0, 0
    goal = shares[0] * total
    for w in weights:
        while k + 1 < len(shares) and run + w / 2.0 > goal:
            k += 1
            goal += shares[k] * total
        owner.append(k)
        run += w
    return owner


def make_plan(T, topo):
    route, cores = T.tables["ROUTE"], list(T.cores)
    n, nt = len(cores), len(route[0])
    par = [topo.chip(c) & 1 for c in cores]
    fill = [0] * n
    tokens = []
    for r in range(n):
        b, k = topo.chip(cores[r]), cores[r] % 8
        rows = []
        for t in range(nt):
            near, far = [], []
            for e in route[r][t]:
                (near if par[e] == par[r] else far).append((e, fill[e]))
                fill[e] += 1
            rows.append((near, far))
        fo = split([(2 if not f else 1) if nr else 0 for nr, f in rows], [s for _, s in FOLDERS[k]])
        ao = split([1 if f else 0 for nr, f in rows], [s for _, s in AGGREGATORS[k]])
        for t in range(nt):
            tokens.append((r, t, rows[t][0], rows[t][1], 8 * b + FOLDERS[k][fo[t]][0],
                           8 * (b ^ 1) + AGGREGATORS[k][ao[t]][0]))
    pieces = {}
    for r, t, near, far, fc, ac in tokens:
        for group, h in ((near, fc), (far, ac)):
            for e, c in group:
                if cores[e] == h:
                    continue
                lst = pieces.setdefault((h, e), [])
                if lst and lst[-1][1] == c:
                    lst[-1][1] = c + 1
                else:
                    lst.append([c, c + 1])
    top, expect, place = {}, {}, {}
    sends = [[] for _ in range(n)]
    for h, e in sorted(pieces):
        for lo, hi in pieces[(h, e)]:
            at = top.get(h, 0)
            top[h] = at + hi - lo
            sends[e].append((h, lo, at, hi - lo))
            expect[h] = expect.get(h, 0) + engines(topo.mask(cores[e], h))
            for c in range(lo, hi):
                place[(h, e, c)] = at + c - lo
    assert max(top.values()) <= SCRATCH["land"][1][1]

    def src(h, group):
        return [("zs", c) if cores[e] == h else ("land", place[(h, e, c)]) for e, c in group]

    jobs = {}
    done, has_m = [0] * n, [[False] * nt for _ in range(n)]
    for r, t, near, far, fc, ac in tokens:
        if not far:
            out = [(fc, near[:2], "S"), (fc, near[2:], "M")]
        elif not near:
            out = [(ac, far, "S")]
        else:
            out = [(fc, near, "S"), (ac, far, "M")]
        for h, group, buf in out:
            jobs.setdefault(h, []).append((src(h, group), cores[r], buf, t))
            done[r] += 1
            if buf == "M":
                has_m[r][t] = True
    runs = []
    for r in range(n):
        rr, t = [], 0
        while t < nt:
            if has_m[r][t]:
                a = t
                while t < nt and has_m[r][t]:
                    t += 1
                rr.append((a, t))
            else:
                t += 1
        runs.append(rr)
    return {"sends": sends, "jobs": jobs, "expect": expect, "done": done, "runs": runs}


def rank_program(g, core, T, topo):
    if "p" not in PLAN:
        PLAN["p"] = make_plan(T, topo)
    plan = PLAN["p"]
    rank = T.rank_of(core)
    sent = 0

    if rank is not None:
        g.dma_start(T.zs[:], T.z[:]).then_inc(T.sem.loaded, 16)
        g.wait_ge(T.sem.loaded, 16)
        for dst, zo, lo, w in plan["sends"][rank]:
            rid, pid, _ = topo.addr(dst)
            m = topo.mask(core, dst)
            g.remote_dma(T.land[:, lo:lo + w], T.zs[:, zo:zo + w], T.sem.arrived, T.sem.sent, pid, rid, m)
            sent += engines(m)

    if core in plan["jobs"]:
        g.wait_ge(T.sem.arrived, plan["expect"][core])
        width = min(engines(topo.mask(core, j[1])) for j in plan["jobs"][core])
        for nsrc in (1, 2, 3):
            some = [j for j in plan["jobs"][core] if len(j[0]) == nsrc]
            while some:
                batch, some = some[:width], some[width:]
                trs = []
                for i, (srcs, dst, buf, col) in enumerate(batch):
                    rid, pid, _ = topo.addr(dst)
                    trs.append(RemoteDMATransfer(dst_ids=[DstId(rid=rid, pnc=pid)], dma_engine_mask=1 << i,
                                                 remote_sem=T.sem.done, srcs=[T[b][:, c:c + 1] for b, c in srcs],
                                                 dsts=[T[buf][:, col:col + 1]], alu_op=1 if nsrc > 1 else 0))
                g.remote_dma_fused(trs, local_sem=T.sem.sent)
                sent += len(trs)

    if rank is not None:
        g.wait_ge(T.sem.done, plan["done"][rank])
        for a, b in plan["runs"][rank]:
            g.dma_start(T.S[:, a:b], T.M[:, a:b], accum_op=AluOpType.add).then_inc(T.sem.added, 16)
        g.wait_ge(T.sem.added, 16 * len(plan["runs"][rank]))
        g.dma_start(T.y[:], T.S[:]).then_inc(T.sem.stored, 16)
        g.wait_ge(T.sem.stored, 16)

    if sent:
        g.wait_ge(T.sem.sent, sent)
